import numpy as np
import ml_dtypes


def mxq(x, axis, fmt="e4m3"):
    dtype, down = {"e4m3": (ml_dtypes.float8_e4m3fn, 7), "e5m2": (ml_dtypes.float8_e5m2, 14)}[fmt]
    v = np.moveaxis(np.asarray(x, np.float32).astype(ml_dtypes.bfloat16).astype(np.float64), axis, -1)
    blocks = v.reshape(v.shape[:-1] + (-1, 32))
    amax = np.abs(blocks).max(-1, keepdims=True)
    byte = np.maximum(np.where(amax > 0, np.frexp(amax)[1] - 1 + 127, 0) - down, 1)
    scale = np.exp2(byte - 127.0)
    codes = (blocks / scale).astype(np.float32).astype(dtype).astype(np.float64)
    return np.moveaxis((codes * scale).reshape(v.shape), -1, axis)


WIDE = False


def mx_kscale(k):
    if not WIDE:
        return np.ones(k)
    levels = np.array([10, -10, 5, -5, 0])
    if k % 512:
        return np.exp2(np.random.permutation(np.resize(levels, k // 32))).repeat(32)
    a = np.empty((k // 512, 16))
    for p in range(k // 512):
        a[p, :8] = np.random.permutation(np.resize(levels, 8))
        for g in range(8):
            far = levels[np.abs(levels - a[p, g]) >= 10]
            a[p, g + 8] = far[np.random.randint(len(far))]
    return np.exp2(a.ravel()).repeat(32)


def f64(x):
    return np.asarray(x).astype(np.float64)


def striped(idx):
    return np.tile(idx.reshape(-1, 16).T, (8, 1)).astype(np.uint16)


def unstriped(offs):
    return offs[:16].T.reshape(-1).astype(np.int64)


def pack_weight(w):
    k, n = w.shape
    w = f64(np.asarray(w, np.float32).astype(ml_dtypes.bfloat16)).reshape(k // 32, 32, n)
    amax = np.abs(w).max(1)
    byte = np.clip(np.where(amax > 0, np.frexp(amax)[1] - 1 + 127 - 7, 1), 1, 254)
    scaled = (w * np.exp2(127.0 - byte)[:, None, :]).reshape(k, n).astype(np.float32)
    words = np.ascontiguousarray(scaled.reshape(k // 512, 128, 4, n).transpose(0, 1, 3, 2)).astype(ml_dtypes.float8_e4m3fn).view(np.uint8)
    return words, np.ascontiguousarray(byte.astype(np.uint8).reshape(k // 512, 16, n))


def unpack_weight(words, scales):
    g, p, n, _ = words.shape
    vals = np.ascontiguousarray(words).view(ml_dtypes.float8_e4m3fn).astype(np.float64) * np.repeat(np.exp2(scales.astype(np.float64) - 127.0), 8, axis=1)[..., None]
    return vals.transpose(0, 1, 3, 2).reshape(g * 512, n)


def sigmoid(v):
    return 1.0 / (1.0 + np.exp(-np.maximum(v, -700.0)))


K, T, S, N, U = 512, 2048, 512, 256, 1024
P = 2 ** 7


def setup_inputs():
    n = np.random.standard_normal
    s = mx_kscale(K)[:, None]
    packed_xT = pack_weight(n((K, T)) * s)
    return {
        "x_words": packed_xT[0],
        "x_scales": packed_xT[1],
        "w1": (n((K, N)) / np.sqrt(K) / s).astype(np.float32),
        "w2": (n((K, N)) / np.sqrt(K) / s).astype(np.float32),
        "band": (np.tile(np.random.uniform(0.5, 1.0, S), (P, 1))).astype(np.float32),
        "dist": (n((N, U)) * 0.5).astype(np.float32),
        "wgt": (np.random.uniform(0.2, 3.0, (N, U))).astype(np.float32),
        "offs": striped(np.random.permutation(T)[:S]),
        "vox": striped(np.random.permutation(U)[:S]),
    }


def reference(x_words, x_scales, w1, w2, band, dist, wgt, offs, vox):
    wg = f64(wgt)[:, unstriped(vox)]
    dg = f64(dist)[:, unstriped(vox)]
    xq = unpack_weight(x_words, x_scales)[:, unstriped(offs)]
    yw = mxq(f64(w2), 0, "e4m3").T @ xq
    wn = sigmoid(yw)
    yd = mxq(f64(w1), 0, "e4m3").T @ xq
    td = np.maximum(np.minimum(yd, f64(band)[:1]), -1.0 * f64(band)[:1])
    nd = (wg * dg + wn * td) / (wg + wn)
    out = f64(dist).copy()
    out[:, unstriped(vox)] = nd
    return out

@@ -1,0 +1,198 @@
+from contextlib import ExitStack
+
+import concourse.mybir as mybir
+from concourse.masks import make_identity
+
+K, T, S, N, U = 512, 2048, 512, 256, 1024
+FLOPS = 2 * 2 * K * N * S
+
+F32 = mybir.dt.float32
+BF16 = mybir.dt.bfloat16
+I32 = mybir.dt.int32
+U32 = mybir.dt.uint32
+U16 = mybir.dt.uint16
+U8 = mybir.dt.uint8
+FP8X4 = mybir.dt.float8_e4m3fn_x4
+ALU = mybir.AluOpType
+ACT = mybir.ActivationFunctionType
+
+P = 128
+PACK = 4
+BLOCKS = N // P
+JT = S // P
+
+
+def tile_picked_ytsdf_dist_p_kernel(
+    tc, x_words, x_scales, w1, w2, band, dist, wgt, offs, vox, out
+):
+    nc = tc.nc
+    with ExitStack() as ctx:
+        sb = ctx.enter_context(tc.tile_pool(name="sb", bufs=1))
+        ps = ctx.enter_context(tc.psum_pool(name="ps", bufs=1))
+
+        offs_t = sb.tile([P, S // 16], U16, name="offs_t")
+        vox_t = sb.tile([P, S // 16], U16, name="vox_t")
+        xw = sb.tile([P, T], I32, name="xw", tag="slot_x", align_bytes=64)
+        xs = sb.tile([P, T], U8, name="xs", tag="slot_s", align_bytes=64)
+        band_rows = sb.tile([P, P], F32, name="band_rows")
+        ident = sb.tile([P, P], F32, name="ident")
+        warm = sb.tile([P, 2], F32, name="warm")
+
+        nc.gpsimd.memset(xs[:].bitcast(I32), 0)
+        nc.vector.memset(band_rows[:], 0.0)
+        make_identity(nc, ident[:])
+
+        nc.sync.dma_start(offs_t[:], offs)
+        nc.sync.dma_start(vox_t[:], vox)
+        nc.sync.dma_start(xw[:], x_words[0].rearrange("p c r -> p (c r)").bitcast(I32))
+        for q in range(4):
+            nc.scalar.dma_start(
+                xs[32 * q : 32 * q + 4, :].bitcast(I32), x_scales[0, 4 * q : 4 * q + 4, :].bitcast(I32)
+            )
+        nc.scalar.activation(warm[:, 0:1], band_rows[:, P - 1 : P], ACT.Sigmoid)
+        nc.sync.dma_start(band_rows[0:JT, :], band[0:1, :].rearrange("o (t c) -> (o t) c", t=JT))
+        w_raw = {}
+        for name, w in (("w2", w2), ("w1", w1)):
+            w_raw[name] = sb.tile([P, PACK, N], F32, name=name + "_raw", tag="slot_" + name, align_bytes=64)
+            nc.sync.dma_start(w_raw[name][:], w.rearrange("(p j) n -> p j n", j=PACK))
+        wgt_t, dist_t = {}, {}
+
+        def load_rows(tiles, src, b, name, slot):
+            tiles[b] = sb.tile([P, U], F32, name=name, tag=slot, align_bytes=64)
+            nc.sync.dma_start(tiles[b][:], src[b * P : (b + 1) * P, :])
+
+        load_rows(wgt_t, wgt, 0, "wgt0", "slot_wgt0")
+
+        band_ps = ps.tile([P, P], F32, name="band_ps")
+        nc.tensor.transpose(band_ps[:], band_rows[:], ident[:])
+        hi = sb.tile([P, JT], F32, name="hi")
+        lo = sb.tile([P, JT], F32, name="lo")
+        nc.scalar.activation(hi[:], band_ps[:, 0:JT], ACT.Copy)
+        nc.scalar.activation(lo[:], band_ps[:, 0:JT], ACT.Copy, scale=-1.0)
+
+        gs = sb.tile([P, S], U8, name="gs", align_bytes=64)
+        gw = sb.tile([P, S], U32, name="gw", align_bytes=64)
+        nc.vector.tensor_copy(gs[:], xs[:].indirect(offs_t[:]))
+        load_rows(wgt_t, wgt, 1, "wgt1", "slot_s")
+        nc.vector.tensor_copy(gw[:], xw[:].bitcast(U32).indirect(offs_t[:]))
+
+        load_rows(dist_t, dist, 0, "dist0", "slot_x")
+        codes, scales = {}, {}
+        for name in ("w2", "w1"):
+            grouped = sb.tile([P, N, PACK], BF16, name=name + "_bf", align_bytes=64)
+            dst = grouped[:].rearrange("p (c i) t -> p c t i", i=4)
+            src = w_raw[name][:].rearrange("p t (c i) -> p c t i", i=4)
+            nc.vector.tensor_copy(dst, src)
+            if name == "w2":
+                load_rows(dist_t, dist, 1, "dist1", "slot_w2")
+            codes[name] = sb.tile([P, N], U32, name=name + "_codes", align_bytes=64)
+            scales[name] = sb.tile([P, N], U8, name=name + "_scales", align_bytes=64)
+            nc.vector.quantize_mx(
+                out=codes[name][:].bitcast(FP8X4),
+                scales=scales[name][:],
+                in_=grouped[:].rearrange("p n t -> p (n t)"),
+            )
+            if name == "w2":
+                wn = []
+                for b in range(BLOCKS):
+                    yw = ps.tile([P, S], F32, name="yw%d" % b)
+                    cols = slice(b * P, (b + 1) * P)
+                    nc.tensor.matmul_mx(
+                        out=yw[:],
+                        lhsT=codes[name][:, cols].bitcast(FP8X4),
+                        lhsT_scale=scales[name][:, cols],
+                        rhs=gw[:].bitcast(FP8X4),
+                        rhs_scale=gs[:],
+                        start=True,
+                        stop=True,
+                    )
+                    wn.append(sb.tile([P, S], F32, name="wn%d" % b))
+                    nc.scalar.activation(wn[b][:], yw[:], ACT.Sigmoid)
+
+        ydT = [ps.tile([P, 2, N], F32, name="ydT%d" % h) for h in range(JT // 2)]
+        for t in range(JT):
+            cols = slice(t * P, (t + 1) * P)
+            nc.tensor.matmul_mx(
+                out=ydT[t // 2][:, t % 2, :],
+                lhsT=gw[:, cols].bitcast(FP8X4),
+                lhsT_scale=gs[:, cols],
+                rhs=codes["w1"][:].bitcast(FP8X4),
+                rhs_scale=scales["w1"][:],
+                start=True,
+                stop=True,
+            )
+
+        def new(name, b, tag=None):
+            return sb.tile([P, S], F32, name="%s%d" % (name, b), tag=tag or "%s%d" % (name, b))
+
+        den, sgn, root, rec, td_ps, td, diff, swn, share, step = ({} for unused in range(10))
+
+        def denominator(b):
+            den[b] = new("den", b)
+            nc.vector.tensor_tensor(den[b][:], wgt_t[b][:].indirect(vox_t[:]), wn[b][:], ALU.add)
+
+        def sign(b):
+            sgn[b] = new("sgn", b)
+            nc.scalar.activation(sgn[b][:], den[b][:], ACT.Sign)
+
+        def inverse_root(b):
+            root[b] = new("root", b)
+            nc.scalar.activation(root[b][:], den[b][:], ACT.Abs_reciprocal_sqrt)
+
+        def square(b):
+            rec[b] = new("rec", b)
+            nc.scalar.activation(rec[b][:], root[b][:], ACT.Square)
+
+        def leave_psum(b):
+            td[b] = new("td", b)
+            nc.scalar.activation(td[b][:], td_ps[b][:], ACT.Copy)
+
+        def signed_weight(b):
+            swn[b] = new("swn", b)
+            nc.vector.tensor_tensor(swn[b][:], sgn[b][:], wn[b][:], ALU.mult)
+
+        def difference(b):
+            diff[b] = new("diff", b)
+            nc.vector.tensor_tensor(diff[b][:], dist_t[b][:].indirect(vox_t[:]), td[b][:], ALU.subtract)
+
+        def new_share(b):
+            share[b] = new("share", b)
+            nc.vector.scalar_tensor_tensor(share[b][:], swn[b][:], -1.0, rec[b][:], ALU.mult, ALU.mult)
+
+        def make_step(b, tag=None):
+            step[b] = new("step", b, tag)
+            nc.vector.scalar_tensor_tensor(step[b][:], share[b][:], 1.0, diff[b][:], ALU.add, ALU.mult)
+
+        def put_back(b):
+            nc.vector.tensor_tensor(dist_t[b][:].indirect(vox_t[:]), step[b][:], td[b][:], ALU.add)
+            nc.sync.dma_start(out[b * P : (b + 1) * P, :], dist_t[b][:])
+
+        denominator(0)
+        tdT = sb.tile([P, JT, N], F32, name="tdT")
+        for t in range(JT):
+            nc.vector.tensor_scalar(
+                tdT[:, t, :], ydT[t // 2][:, t % 2, :], hi[:, t : t + 1], lo[:, t : t + 1], ALU.min, ALU.max
+            )
+        denominator(1)
+        for b in range(BLOCKS):
+            td_ps[b] = ps.tile([P, S], F32, name="td_ps%d" % b)
+            for t in range(JT):
+                nc.tensor.transpose(td_ps[b][:, t * P : (t + 1) * P], tdT[:, t, b * P : (b + 1) * P], ident[:])
+        inverse_root(0)
+        sign(0)
+        leave_psum(0)
+        sign(1)
+        square(0)
+        leave_psum(1)
+        inverse_root(1)
+        square(1)
+        signed_weight(0)
+        difference(0)
+        signed_weight(1)
+        new_share(0)
+        difference(1)
+        new_share(1)
+        make_step(0, "root1")
+        make_step(1)
+        put_back(0)
+        put_back(1)

@@ -39,22 +39,26 @@ def tile_picked_ytsdf_dist_p_kernel(
         warm = sb.tile([P, 2], F32, name="warm")
 
         nc.gpsimd.memset(xs[:].bitcast(I32), 0)
-        nc.vector.memset(band_rows[:], 0.0)
         make_identity(nc, ident[:])
+        nc.gpsimd.memset(band_rows[:], 0.0)
 
         nc.sync.dma_start(offs_t[:], offs)
         nc.sync.dma_start(vox_t[:], vox)
-        nc.sync.dma_start(xw[:], x_words[0].rearrange("p c r -> p (c r)").bitcast(I32))
+        w_raw = {}
+
+        def load_weights(name, w):
+            w_raw[name] = sb.tile([P, PACK, N], F32, name=name + "_raw", tag="slot_" + name, align_bytes=64)
+            nc.sync.dma_start(w_raw[name][:], w.rearrange("(p j) n -> p j n", j=PACK))
+
+        load_weights("w2", w2)
         for q in range(4):
             nc.scalar.dma_start(
                 xs[32 * q : 32 * q + 4, :].bitcast(I32), x_scales[0, 4 * q : 4 * q + 4, :].bitcast(I32)
             )
-        nc.scalar.activation(warm[:, 0:1], band_rows[:, P - 1 : P], ACT.Sigmoid)
+        nc.scalar.activation(warm[:, 0:1], ident[:, 0:1], ACT.Sigmoid)
         nc.sync.dma_start(band_rows[0:JT, :], band[0:1, :].rearrange("o (t c) -> (o t) c", t=JT))
-        w_raw = {}
-        for name, w in (("w2", w2), ("w1", w1)):
-            w_raw[name] = sb.tile([P, PACK, N], F32, name=name + "_raw", tag="slot_" + name, align_bytes=64)
-            nc.sync.dma_start(w_raw[name][:], w.rearrange("(p j) n -> p j n", j=PACK))
+        nc.sync.dma_start(xw[:], x_words[0].rearrange("p c r -> p (c r)").bitcast(I32))
+        load_weights("w1", w1)
         wgt_t, dist_t = {}, {}
 
         def load_rows(tiles, src, b, name, slot):
@@ -70,21 +74,14 @@ def tile_picked_ytsdf_dist_p_kernel(
         nc.scalar.activation(hi[:], band_ps[:, 0:JT], ACT.Copy)
         nc.scalar.activation(lo[:], band_ps[:, 0:JT], ACT.Copy, scale=-1.0)
 
-        gs = sb.tile([P, S], U8, name="gs", align_bytes=64)
-        gw = sb.tile([P, S], U32, name="gw", align_bytes=64)
-        nc.vector.tensor_copy(gs[:], xs[:].indirect(offs_t[:]))
-        load_rows(wgt_t, wgt, 1, "wgt1", "slot_s")
-        nc.vector.tensor_copy(gw[:], xw[:].bitcast(U32).indirect(offs_t[:]))
-
-        load_rows(dist_t, dist, 0, "dist0", "slot_x")
         codes, scales = {}, {}
-        for name in ("w2", "w1"):
+
+        def quantise(name):
             grouped = sb.tile([P, N, PACK], BF16, name=name + "_bf", align_bytes=64)
-            dst = grouped[:].rearrange("p (c i) t -> p c t i", i=4)
-            src = w_raw[name][:].rearrange("p t (c i) -> p c t i", i=4)
-            nc.vector.tensor_copy(dst, src)
-            if name == "w2":
-                load_rows(dist_t, dist, 1, "dist1", "slot_w2")
+            nc.vector.tensor_copy(
+                grouped[:].rearrange("p (c i) t -> p c t i", i=4),
+                w_raw[name][:].rearrange("p t (c i) -> p c t i", i=4),
+            )
             codes[name] = sb.tile([P, N], U32, name=name + "_codes", align_bytes=64)
             scales[name] = sb.tile([P, N], U8, name=name + "_scales", align_bytes=64)
             nc.vector.quantize_mx(
@@ -92,22 +89,33 @@ def tile_picked_ytsdf_dist_p_kernel(
                 scales=scales[name][:],
                 in_=grouped[:].rearrange("p n t -> p (n t)"),
             )
-            if name == "w2":
-                wn = []
-                for b in range(BLOCKS):
-                    yw = ps.tile([P, S], F32, name="yw%d" % b)
-                    cols = slice(b * P, (b + 1) * P)
-                    nc.tensor.matmul_mx(
-                        out=yw[:],
-                        lhsT=codes[name][:, cols].bitcast(FP8X4),
-                        lhsT_scale=scales[name][:, cols],
-                        rhs=gw[:].bitcast(FP8X4),
-                        rhs_scale=gs[:],
-                        start=True,
-                        stop=True,
-                    )
-                    wn.append(sb.tile([P, S], F32, name="wn%d" % b))
-                    nc.scalar.activation(wn[b][:], yw[:], ACT.Sigmoid)
+
+        gs = sb.tile([P, S], U8, name="gs", align_bytes=64)
+        gw = sb.tile([P, S], U32, name="gw", align_bytes=64)
+        quantise("w2")
+        load_rows(wgt_t, wgt, 1, "wgt1", "slot_w2")
+        nc.vector.tensor_copy(gs[:], xs[:].indirect(offs_t[:]))
+        load_rows(dist_t, dist, 0, "dist0", "slot_s")
+        nc.vector.tensor_copy(gw[:], xw[:].bitcast(U32).indirect(offs_t[:]))
+        load_rows(dist_t, dist, 1, "dist1", "slot_x")
+
+        wn = []
+        for b in range(BLOCKS):
+            yw = ps.tile([P, S], F32, name="yw%d" % b)
+            cols = slice(b * P, (b + 1) * P)
+            nc.tensor.matmul_mx(
+                out=yw[:],
+                lhsT=codes["w2"][:, cols].bitcast(FP8X4),
+                lhsT_scale=scales["w2"][:, cols],
+                rhs=gw[:].bitcast(FP8X4),
+                rhs_scale=gs[:],
+                start=True,
+                stop=True,
+            )
+            wn.append(sb.tile([P, S], F32, name="wn%d" % b))
+            nc.scalar.activation(wn[b][:], yw[:], ACT.Sigmoid)
+        nc.scalar.activation(warm[:, 1:2], wn[1][:, 0:1], ACT.Abs_reciprocal_sqrt)
+        quantise("w1")
 
         ydT = [ps.tile([P, 2, N], F32, name="ydT%d" % h) for h in range(JT // 2)]
         for t in range(JT):

@@ -1,7 +1,6 @@
 from contextlib import ExitStack
 
 import concourse.mybir as mybir
-from concourse.masks import make_identity
 
 K, T, S, N, U = 512, 2048, 512, 256, 1024
 FLOPS = 2 * 2 * K * N * S
@@ -32,15 +31,26 @@ def tile_picked_ytsdf_dist_p_kernel(
 
         offs_t = sb.tile([P, S // 16], U16, name="offs_t")
         vox_t = sb.tile([P, S // 16], U16, name="vox_t")
-        xw = sb.tile([P, T], I32, name="xw", tag="slot_x", align_bytes=64)
         xs = sb.tile([P, T], U8, name="xs", tag="slot_s", align_bytes=64)
         band_rows = sb.tile([P, P], F32, name="band_rows")
         ident = sb.tile([P, P], F32, name="ident")
         warm = sb.tile([P, 2], F32, name="warm")
 
-        nc.gpsimd.memset(xs[:].bitcast(I32), 0)
-        make_identity(nc, ident[:])
-        nc.gpsimd.memset(band_rows[:], 0.0)
+        nc.vector.memset(xs[:].bitcast(I32), 0)
+        ones = sb.tile([P, P], F32, name="ones", tag="slot_x", align_bytes=64)
+        column = sb.tile([P, P], F32, name="column", align_bytes=64)
+        turned = sb.tile([P, P], F32, name="turned", align_bytes=64)
+        nc.vector.memset(ones[:], 1.0)
+        nc.vector.tensor_tensor_scan(column[:], ones[:], ones[:], 0.0, ALU.mult, ALU.add)
+        warm_in = sb.tile([P, 1], F32, name="warm_in", tag="slot_w1", align_bytes=64)
+        nc.vector.memset(warm_in[:], 0.0)
+        nc.vector.memset(band_rows[:], 0.0)
+        nc.vector.transpose(turned[:], column[:])
+        for q in range(4):
+            rows = slice(32 * q, 32 * q + 32)
+            nc.vector.tensor_scalar(
+                ident[rows, :], column[rows, :], turned[rows, 32 * q : 32 * q + 1], None, ALU.is_equal
+            )
 
         nc.sync.dma_start(offs_t[:], offs)
         nc.sync.dma_start(vox_t[:], vox)
@@ -52,12 +62,13 @@ def tile_picked_ytsdf_dist_p_kernel(
 
         load_weights("w2", w2)
         for q in range(4):
-            nc.scalar.dma_start(
+            nc.sync.dma_start(
                 xs[32 * q : 32 * q + 4, :].bitcast(I32), x_scales[0, 4 * q : 4 * q + 4, :].bitcast(I32)
             )
-        nc.scalar.activation(warm[:, 0:1], ident[:, 0:1], ACT.Sigmoid)
-        nc.sync.dma_start(band_rows[0:JT, :], band[0:1, :].rearrange("o (t c) -> (o t) c", t=JT))
+        nc.scalar.activation(warm[:, 0:1], warm_in[:], ACT.Sigmoid)
+        xw = sb.tile([P, T], I32, name="xw", tag="slot_x", align_bytes=64)
         nc.sync.dma_start(xw[:], x_words[0].rearrange("p c r -> p (c r)").bitcast(I32))
+        nc.sync.dma_start(band_rows[0:JT, :], band[0:1, :].rearrange("o (t c) -> (o t) c", t=JT))
         load_weights("w1", w1)
         wgt_t, dist_t = {}, {}
 
@@ -65,7 +76,6 @@ def tile_picked_ytsdf_dist_p_kernel(
             tiles[b] = sb.tile([P, U], F32, name=name, tag=slot, align_bytes=64)
             nc.sync.dma_start(tiles[b][:], src[b * P : (b + 1) * P, :])
 
-        load_rows(wgt_t, wgt, 0, "wgt0", "slot_wgt0")
 
         band_ps = ps.tile([P, P], F32, name="band_ps")
         nc.tensor.transpose(band_ps[:], band_rows[:], ident[:])
@@ -93,11 +103,11 @@ def tile_picked_ytsdf_dist_p_kernel(
         gs = sb.tile([P, S], U8, name="gs", align_bytes=64)
         gw = sb.tile([P, S], U32, name="gw", align_bytes=64)
         quantise("w2")
-        load_rows(wgt_t, wgt, 1, "wgt1", "slot_w2")
+        load_rows(wgt_t, wgt, 0, "wgt0", "slot_w2")
         nc.vector.tensor_copy(gs[:], xs[:].indirect(offs_t[:]))
-        load_rows(dist_t, dist, 0, "dist0", "slot_s")
+        load_rows(wgt_t, wgt, 1, "wgt1", "slot_s")
         nc.vector.tensor_copy(gw[:], xw[:].bitcast(U32).indirect(offs_t[:]))
-        load_rows(dist_t, dist, 1, "dist1", "slot_x")
+        load_rows(dist_t, dist, 0, "dist0", "slot_x")
 
         wn = []
         for b in range(BLOCKS):
@@ -114,8 +124,9 @@ def tile_picked_ytsdf_dist_p_kernel(
             )
             wn.append(sb.tile([P, S], F32, name="wn%d" % b))
             nc.scalar.activation(wn[b][:], yw[:], ACT.Sigmoid)
-        nc.scalar.activation(warm[:, 1:2], wn[1][:, 0:1], ACT.Abs_reciprocal_sqrt)
+        nc.scalar.activation(warm[:, 1:2], wn[1][:, 0:1], ACT.Abs_reciprocal_sqrt, scale=lo[:, 0:1])
         quantise("w1")
+        load_rows(dist_t, dist, 1, "dist1", "slot_w1")
 
         ydT = [ps.tile([P, 2, N], F32, name="ydT%d" % h) for h in range(JT // 2)]
         for t in range(JT):

@@ -16,9 +16,12 @@ ALU = mybir.AluOpType
 ACT = mybir.ActivationFunctionType
 
 P = 128
+QUAD = 32
 PACK = 4
 BLOCKS = N // P
-JT = S // P
+ENTRY_TILES = S // P
+PER_BANK = 2
+LINE = 4
 
 
 def tile_picked_ytsdf_dist_p_kernel(
@@ -34,63 +37,61 @@ def tile_picked_ytsdf_dist_p_kernel(
         xs = sb.tile([P, T], U8, name="xs", tag="slot_s", align_bytes=64)
         band_rows = sb.tile([P, P], F32, name="band_rows")
         ident = sb.tile([P, P], F32, name="ident")
-        warm = sb.tile([P, 2], F32, name="warm")
 
         nc.vector.memset(xs[:].bitcast(I32), 0)
+
         ones = sb.tile([P, P], F32, name="ones", tag="slot_x", align_bytes=64)
         column = sb.tile([P, P], F32, name="column", align_bytes=64)
-        turned = sb.tile([P, P], F32, name="turned", align_bytes=64)
+        turned = sb.tile([P, P], F32, name="turned", tag="slot_w1", align_bytes=64)
         nc.vector.memset(ones[:], 1.0)
         nc.vector.tensor_tensor_scan(column[:], ones[:], ones[:], 0.0, ALU.mult, ALU.add)
-        warm_in = sb.tile([P, 1], F32, name="warm_in", tag="slot_w1", align_bytes=64)
-        nc.vector.memset(warm_in[:], 0.0)
         nc.vector.memset(band_rows[:], 0.0)
         nc.vector.transpose(turned[:], column[:])
-        for q in range(4):
-            rows = slice(32 * q, 32 * q + 32)
+        for q in range(P // QUAD):
+            rows = slice(QUAD * q, QUAD * (q + 1))
             nc.vector.tensor_scalar(
-                ident[rows, :], column[rows, :], turned[rows, 32 * q : 32 * q + 1], None, ALU.is_equal
+                ident[rows, :], column[rows, :], turned[rows, QUAD * q : QUAD * q + 1], None, ALU.is_equal
             )
 
-        nc.sync.dma_start(offs_t[:], offs)
-        nc.sync.dma_start(vox_t[:], vox)
-        w_raw = {}
+        w_raw, wgt_t, dist_t = {}, {}, {}
 
         def load_weights(name, w):
             w_raw[name] = sb.tile([P, PACK, N], F32, name=name + "_raw", tag="slot_" + name, align_bytes=64)
             nc.sync.dma_start(w_raw[name][:], w.rearrange("(p j) n -> p j n", j=PACK))
 
-        load_weights("w2", w2)
-        for q in range(4):
-            nc.sync.dma_start(
-                xs[32 * q : 32 * q + 4, :].bitcast(I32), x_scales[0, 4 * q : 4 * q + 4, :].bitcast(I32)
-            )
-        nc.scalar.activation(warm[:, 0:1], warm_in[:], ACT.Sigmoid)
-        xw = sb.tile([P, T], I32, name="xw", tag="slot_x", align_bytes=64)
-        nc.sync.dma_start(xw[:], x_words[0].rearrange("p c r -> p (c r)").bitcast(I32))
-        nc.sync.dma_start(band_rows[0:JT, :], band[0:1, :].rearrange("o (t c) -> (o t) c", t=JT))
-        load_weights("w1", w1)
-        wgt_t, dist_t = {}, {}
-
         def load_rows(tiles, src, b, name, slot):
-            tiles[b] = sb.tile([P, U], F32, name=name, tag=slot, align_bytes=64)
+            tiles[b] = sb.tile([P, U], F32, name="%s%d" % (name, b), tag=slot, align_bytes=64)
             nc.sync.dma_start(tiles[b][:], src[b * P : (b + 1) * P, :])
 
+        nc.sync.dma_start(offs_t[:], offs)
+        nc.sync.dma_start(vox_t[:], vox)
+        load_weights("w2", w2)
+        for q in range(P // QUAD):
+            nc.sync.dma_start(
+                xs[QUAD * q : QUAD * q + PACK, :].bitcast(I32),
+                x_scales[0, PACK * q : PACK * (q + 1), :].bitcast(I32),
+            )
+        xw = sb.tile([P, T], I32, name="xw", tag="slot_x", align_bytes=64)
+        nc.sync.dma_start(xw[:], x_words[0].rearrange("p c r -> p (c r)").bitcast(I32))
+        nc.sync.dma_start(
+            band_rows[0:ENTRY_TILES, :], band[0:1, :].rearrange("o (t c) -> (o t) c", t=ENTRY_TILES)
+        )
+        load_weights("w1", w1)
 
         band_ps = ps.tile([P, P], F32, name="band_ps")
         nc.tensor.transpose(band_ps[:], band_rows[:], ident[:])
-        hi = sb.tile([P, JT], F32, name="hi")
-        lo = sb.tile([P, JT], F32, name="lo")
-        nc.scalar.activation(hi[:], band_ps[:, 0:JT], ACT.Copy)
-        nc.scalar.activation(lo[:], band_ps[:, 0:JT], ACT.Copy, scale=-1.0)
+        hi = sb.tile([P, ENTRY_TILES], F32, name="hi")
+        lo = sb.tile([P, ENTRY_TILES], F32, name="lo")
+        nc.scalar.activation(hi[:], band_ps[:, 0:ENTRY_TILES], ACT.Copy)
+        nc.scalar.activation(lo[:], band_ps[:, 0:ENTRY_TILES], ACT.Copy, scale=-1.0)
 
         codes, scales = {}, {}
 
         def quantise(name):
             grouped = sb.tile([P, N, PACK], BF16, name=name + "_bf", align_bytes=64)
             nc.vector.tensor_copy(
-                grouped[:].rearrange("p (c i) t -> p c t i", i=4),
-                w_raw[name][:].rearrange("p t (c i) -> p c t i", i=4),
+                grouped[:].rearrange("p (c i) t -> p c t i", i=LINE),
+                w_raw[name][:].rearrange("p t (c i) -> p c t i", i=LINE),
             )
             codes[name] = sb.tile([P, N], U32, name=name + "_codes", align_bytes=64)
             scales[name] = sb.tile([P, N], U8, name=name + "_scales", align_bytes=64)
@@ -100,16 +101,19 @@ def tile_picked_ytsdf_dist_p_kernel(
                 in_=grouped[:].rearrange("p n t -> p (n t)"),
             )
 
-        gs = sb.tile([P, S], U8, name="gs", align_bytes=64)
-        gw = sb.tile([P, S], U32, name="gw", align_bytes=64)
+        x_bytes = sb.tile([P, S], U8, name="x_bytes", align_bytes=64)
+        x_codes = sb.tile([P, S], U32, name="x_codes", align_bytes=64)
         quantise("w2")
-        load_rows(wgt_t, wgt, 0, "wgt0", "slot_w2")
-        nc.vector.tensor_copy(gs[:], xs[:].indirect(offs_t[:]))
-        load_rows(wgt_t, wgt, 1, "wgt1", "slot_s")
-        nc.vector.tensor_copy(gw[:], xw[:].bitcast(U32).indirect(offs_t[:]))
-        load_rows(dist_t, dist, 0, "dist0", "slot_x")
+        load_rows(wgt_t, wgt, 0, "wgt", "slot_w2")
+        nc.vector.tensor_copy(x_bytes[:], xs[:].indirect(offs_t[:]))
+        load_rows(wgt_t, wgt, 1, "wgt", "slot_s")
+        nc.vector.tensor_copy(x_codes[:], xw[:].bitcast(U32).indirect(offs_t[:]))
+        load_rows(dist_t, dist, 0, "dist", "slot_x")
 
-        wn = []
+        def block_tile(name, b, tag=None):
+            return sb.tile([P, S], F32, name="%s%d" % (name, b), tag=tag or "%s%d" % (name, b))
+
+        wn = {}
         for b in range(BLOCKS):
             yw = ps.tile([P, S], F32, name="yw%d" % b)
             cols = slice(b * P, (b + 1) * P)
@@ -117,69 +121,65 @@ def tile_picked_ytsdf_dist_p_kernel(
                 out=yw[:],
                 lhsT=codes["w2"][:, cols].bitcast(FP8X4),
                 lhsT_scale=scales["w2"][:, cols],
-                rhs=gw[:].bitcast(FP8X4),
-                rhs_scale=gs[:],
+                rhs=x_codes[:].bitcast(FP8X4),
+                rhs_scale=x_bytes[:],
                 start=True,
                 stop=True,
             )
-            wn.append(sb.tile([P, S], F32, name="wn%d" % b))
+            wn[b] = block_tile("wn", b)
             nc.scalar.activation(wn[b][:], yw[:], ACT.Sigmoid)
-        nc.scalar.activation(warm[:, 1:2], wn[1][:, 0:1], ACT.Abs_reciprocal_sqrt, scale=lo[:, 0:1])
         quantise("w1")
-        load_rows(dist_t, dist, 1, "dist1", "slot_w1")
+        load_rows(dist_t, dist, 1, "dist", "slot_w1")
 
-        ydT = [ps.tile([P, 2, N], F32, name="ydT%d" % h) for h in range(JT // 2)]
-        for t in range(JT):
+        yd_t = [ps.tile([P, PER_BANK, N], F32, name="yd_t%d" % h) for h in range(ENTRY_TILES // PER_BANK)]
+        for t in range(ENTRY_TILES):
             cols = slice(t * P, (t + 1) * P)
             nc.tensor.matmul_mx(
-                out=ydT[t // 2][:, t % 2, :],
-                lhsT=gw[:, cols].bitcast(FP8X4),
-                lhsT_scale=gs[:, cols],
+                out=yd_t[t // PER_BANK][:, t % PER_BANK, :],
+                lhsT=x_codes[:, cols].bitcast(FP8X4),
+                lhsT_scale=x_bytes[:, cols],
                 rhs=codes["w1"][:].bitcast(FP8X4),
                 rhs_scale=scales["w1"][:],
                 start=True,
                 stop=True,
             )
 
-        def new(name, b, tag=None):
-            return sb.tile([P, S], F32, name="%s%d" % (name, b), tag=tag or "%s%d" % (name, b))
-
         den, sgn, root, rec, td_ps, td, diff, swn, share, step = ({} for unused in range(10))
 
         def denominator(b):
-            den[b] = new("den", b)
+            den[b] = block_tile("den", b)
             nc.vector.tensor_tensor(den[b][:], wgt_t[b][:].indirect(vox_t[:]), wn[b][:], ALU.add)
 
         def sign(b):
-            sgn[b] = new("sgn", b)
+            sgn[b] = block_tile("sgn", b)
             nc.scalar.activation(sgn[b][:], den[b][:], ACT.Sign)
 
         def inverse_root(b):
-            root[b] = new("root", b)
+            root[b] = block_tile("root", b)
             nc.scalar.activation(root[b][:], den[b][:], ACT.Abs_reciprocal_sqrt)
 
         def square(b):
-            rec[b] = new("rec", b)
+            rec[b] = block_tile("rec", b)
             nc.scalar.activation(rec[b][:], root[b][:], ACT.Square)
 
         def leave_psum(b):
-            td[b] = new("td", b)
+            td[b] = block_tile("td", b)
             nc.scalar.activation(td[b][:], td_ps[b][:], ACT.Copy)
 
         def signed_weight(b):
-            swn[b] = new("swn", b)
+            swn[b] = block_tile("swn", b)
             nc.vector.tensor_tensor(swn[b][:], sgn[b][:], wn[b][:], ALU.mult)
 
         def difference(b):
-            diff[b] = new("diff", b)
+            diff[b] = block_tile("diff", b)
             nc.vector.tensor_tensor(diff[b][:], dist_t[b][:].indirect(vox_t[:]), td[b][:], ALU.subtract)
 
         def new_share(b):
-            share[b] = new("share", b)
+            share[b] = block_tile("share", b)
             nc.vector.scalar_tensor_tensor(share[b][:], swn[b][:], -1.0, rec[b][:], ALU.mult, ALU.mult)
 
         def make_step(b, tag=None):
-            step[b] = new("step", b, tag)
+            step[b] = block_tile("step", b, tag)
             nc.vector.scalar_tensor_tensor(step[b][:], share[b][:], 1.0, diff[b][:], ALU.add, ALU.mult)
 
         def put_back(b):
@@ -187,16 +187,22 @@ def tile_picked_ytsdf_dist_p_kernel(
             nc.sync.dma_start(out[b * P : (b + 1) * P, :], dist_t[b][:])
 
         denominator(0)
-        tdT = sb.tile([P, JT, N], F32, name="tdT")
-        for t in range(JT):
+        td_t = sb.tile([P, ENTRY_TILES, N], F32, name="td_t")
+        for t in range(ENTRY_TILES):
             nc.vector.tensor_scalar(
-                tdT[:, t, :], ydT[t // 2][:, t % 2, :], hi[:, t : t + 1], lo[:, t : t + 1], ALU.min, ALU.max
+                td_t[:, t, :],
+                yd_t[t // PER_BANK][:, t % PER_BANK, :],
+                hi[:, t : t + 1],
+                lo[:, t : t + 1],
+                ALU.min,
+                ALU.max,
             )
         denominator(1)
         for b in range(BLOCKS):
             td_ps[b] = ps.tile([P, S], F32, name="td_ps%d" % b)
-            for t in range(JT):
-                nc.tensor.transpose(td_ps[b][:, t * P : (t + 1) * P], tdT[:, t, b * P : (b + 1) * P], ident[:])
+            for t in range(ENTRY_TILES):
+                nc.tensor.transpose(td_ps[b][:, t * P : (t + 1) * P], td_t[:, t, b * P : (b + 1) * P], ident[:])
+
         inverse_root(0)
         sign(0)
         leave_psum(0)
@@ -205,6 +211,7 @@ def tile_picked_ytsdf_dist_p_kernel(
         leave_psum(1)
         inverse_root(1)
         square(1)
+
         signed_weight(0)
         difference(0)
         signed_weight(1)

from contextlib import ExitStack

import concourse.mybir as mybir

K, T, S, N, U = 512, 2048, 512, 256, 1024
FLOPS = 2 * 2 * K * N * S

F32 = mybir.dt.float32
BF16 = mybir.dt.bfloat16
I32 = mybir.dt.int32
U32 = mybir.dt.uint32
U16 = mybir.dt.uint16
U8 = mybir.dt.uint8
FP8X4 = mybir.dt.float8_e4m3fn_x4
ALU = mybir.AluOpType
ACT = mybir.ActivationFunctionType

P = 128
QUAD = 32
PACK = 4
BLOCKS = N // P
ENTRY_TILES = S // P
PER_BANK = 2
LINE = 4


def tile_picked_ytsdf_dist_p_kernel(
    tc, x_words, x_scales, w1, w2, band, dist, wgt, offs, vox, out
):
    nc = tc.nc
    with ExitStack() as ctx:
        sb = ctx.enter_context(tc.tile_pool(name="sb", bufs=1))
        ps = ctx.enter_context(tc.psum_pool(name="ps", bufs=1))

        offs_t = sb.tile([P, S // 16], U16, name="offs_t")
        vox_t = sb.tile([P, S // 16], U16, name="vox_t")
        xs = sb.tile([P, T], U8, name="xs", tag="slot_s", align_bytes=64)
        band_rows = sb.tile([P, P], F32, name="band_rows")
        ident = sb.tile([P, P], F32, name="ident")

        nc.vector.memset(xs[:].bitcast(I32), 0)

        ones = sb.tile([P, P], F32, name="ones", tag="slot_x", align_bytes=64)
        column = sb.tile([P, P], F32, name="column", align_bytes=64)
        turned = sb.tile([P, P], F32, name="turned", tag="slot_w1", align_bytes=64)
        nc.vector.memset(ones[:], 1.0)
        nc.vector.tensor_tensor_scan(column[:], ones[:], ones[:], 0.0, ALU.mult, ALU.add)
        nc.vector.memset(band_rows[:], 0.0)
        nc.vector.transpose(turned[:], column[:])
        for q in range(P // QUAD):
            rows = slice(QUAD * q, QUAD * (q + 1))
            nc.vector.tensor_scalar(
                ident[rows, :], column[rows, :], turned[rows, QUAD * q : QUAD * q + 1], None, ALU.is_equal
            )

        w_raw, wgt_t, dist_t = {}, {}, {}

        def load_weights(name, w):
            w_raw[name] = sb.tile([P, PACK, N], F32, name=name + "_raw", tag="slot_" + name, align_bytes=64)
            nc.sync.dma_start(w_raw[name][:], w.rearrange("(p j) n -> p j n", j=PACK))

        def load_rows(tiles, src, b, name, slot):
            tiles[b] = sb.tile([P, U], F32, name="%s%d" % (name, b), tag=slot, align_bytes=64)
            nc.sync.dma_start(tiles[b][:], src[b * P : (b + 1) * P, :])

        nc.sync.dma_start(offs_t[:], offs)
        nc.sync.dma_start(vox_t[:], vox)
        load_weights("w2", w2)
        for q in range(P // QUAD):
            nc.sync.dma_start(
                xs[QUAD * q : QUAD * q + PACK, :].bitcast(I32),
                x_scales[0, PACK * q : PACK * (q + 1), :].bitcast(I32),
            )
        xw = sb.tile([P, T], I32, name="xw", tag="slot_x", align_bytes=64)
        nc.sync.dma_start(xw[:], x_words[0].rearrange("p c r -> p (c r)").bitcast(I32))
        nc.sync.dma_start(
            band_rows[0:ENTRY_TILES, :], band[0:1, :].rearrange("o (t c) -> (o t) c", t=ENTRY_TILES)
        )
        load_weights("w1", w1)

        band_ps = ps.tile([P, P], F32, name="band_ps")
        nc.tensor.transpose(band_ps[:], band_rows[:], ident[:])
        hi = sb.tile([P, ENTRY_TILES], F32, name="hi")
        lo = sb.tile([P, ENTRY_TILES], F32, name="lo")
        nc.scalar.activation(hi[:], band_ps[:, 0:ENTRY_TILES], ACT.Copy)
        nc.scalar.activation(lo[:], band_ps[:, 0:ENTRY_TILES], ACT.Copy, scale=-1.0)

        codes, scales = {}, {}

        def quantise(name):
            grouped = sb.tile([P, N, PACK], BF16, name=name + "_bf", align_bytes=64)
            nc.vector.tensor_copy(
                grouped[:].rearrange("p (c i) t -> p c t i", i=LINE),
                w_raw[name][:].rearrange("p t (c i) -> p c t i", i=LINE),
            )
            codes[name] = sb.tile([P, N], U32, name=name + "_codes", align_bytes=64)
            scales[name] = sb.tile([P, N], U8, name=name + "_scales", align_bytes=64)
            nc.vector.quantize_mx(
                out=codes[name][:].bitcast(FP8X4),
                scales=scales[name][:],
                in_=grouped[:].rearrange("p n t -> p (n t)"),
            )

        x_bytes = sb.tile([P, S], U8, name="x_bytes", align_bytes=64)
        x_codes = sb.tile([P, S], U32, name="x_codes", align_bytes=64)
        quantise("w2")
        load_rows(wgt_t, wgt, 0, "wgt", "slot_w2")
        nc.vector.tensor_copy(x_bytes[:], xs[:].indirect(offs_t[:]))
        load_rows(wgt_t, wgt, 1, "wgt", "slot_s")
        nc.vector.tensor_copy(x_codes[:], xw[:].bitcast(U32).indirect(offs_t[:]))
        load_rows(dist_t, dist, 0, "dist", "slot_x")

        def block_tile(name, b, tag=None):
            return sb.tile([P, S], F32, name="%s%d" % (name, b), tag=tag or "%s%d" % (name, b))

        wn = {}
        for b in range(BLOCKS):
            yw = ps.tile([P, S], F32, name="yw%d" % b)
            cols = slice(b * P, (b + 1) * P)
            nc.tensor.matmul_mx(
                out=yw[:],
                lhsT=codes["w2"][:, cols].bitcast(FP8X4),
                lhsT_scale=scales["w2"][:, cols],
                rhs=x_codes[:].bitcast(FP8X4),
                rhs_scale=x_bytes[:],
                start=True,
                stop=True,
            )
            wn[b] = block_tile("wn", b)
            nc.scalar.activation(wn[b][:], yw[:], ACT.Sigmoid)
        quantise("w1")
        load_rows(dist_t, dist, 1, "dist", "slot_w1")

        yd_t = [ps.tile([P, PER_BANK, N], F32, name="yd_t%d" % h) for h in range(ENTRY_TILES // PER_BANK)]
        for t in range(ENTRY_TILES):
            cols = slice(t * P, (t + 1) * P)
            nc.tensor.matmul_mx(
                out=yd_t[t // PER_BANK][:, t % PER_BANK, :],
                lhsT=x_codes[:, cols].bitcast(FP8X4),
                lhsT_scale=x_bytes[:, cols],
                rhs=codes["w1"][:].bitcast(FP8X4),
                rhs_scale=scales["w1"][:],
                start=True,
                stop=True,
            )

        den, sgn, root, rec, td_ps, td, diff, swn, share, step = ({} for unused in range(10))

        def denominator(b):
            den[b] = block_tile("den", b)
            nc.vector.tensor_tensor(den[b][:], wgt_t[b][:].indirect(vox_t[:]), wn[b][:], ALU.add)

        def sign(b):
            sgn[b] = block_tile("sgn", b)
            nc.scalar.activation(sgn[b][:], den[b][:], ACT.Sign)

        def inverse_root(b):
            root[b] = block_tile("root", b)
            nc.scalar.activation(root[b][:], den[b][:], ACT.Abs_reciprocal_sqrt)

        def square(b):
            rec[b] = block_tile("rec", b)
            nc.scalar.activation(rec[b][:], root[b][:], ACT.Square)

        def leave_psum(b):
            td[b] = block_tile("td", b)
            nc.scalar.activation(td[b][:], td_ps[b][:], ACT.Copy)

        def signed_weight(b):
            swn[b] = block_tile("swn", b)
            nc.vector.tensor_tensor(swn[b][:], sgn[b][:], wn[b][:], ALU.mult)

        def difference(b):
            diff[b] = block_tile("diff", b)
            nc.vector.tensor_tensor(diff[b][:], dist_t[b][:].indirect(vox_t[:]), td[b][:], ALU.subtract)

        def new_share(b):
            share[b] = block_tile("share", b)
            nc.vector.scalar_tensor_tensor(share[b][:], swn[b][:], -1.0, rec[b][:], ALU.mult, ALU.mult)

        def make_step(b, tag=None):
            step[b] = block_tile("step", b, tag)
            nc.vector.scalar_tensor_tensor(step[b][:], share[b][:], 1.0, diff[b][:], ALU.add, ALU.mult)

        def put_back(b):
            nc.vector.tensor_tensor(dist_t[b][:].indirect(vox_t[:]), step[b][:], td[b][:], ALU.add)
            nc.sync.dma_start(out[b * P : (b + 1) * P, :], dist_t[b][:])

        denominator(0)
        td_t = sb.tile([P, ENTRY_TILES, N], F32, name="td_t")
        for t in range(ENTRY_TILES):
            nc.vector.tensor_scalar(
                td_t[:, t, :],
                yd_t[t // PER_BANK][:, t % PER_BANK, :],
                hi[:, t : t + 1],
                lo[:, t : t + 1],
                ALU.min,
                ALU.max,
            )
        denominator(1)
        for b in range(BLOCKS):
            td_ps[b] = ps.tile([P, S], F32, name="td_ps%d" % b)
            for t in range(ENTRY_TILES):
                nc.tensor.transpose(td_ps[b][:, t * P : (t + 1) * P], td_t[:, t, b * P : (b + 1) * P], ident[:])

        inverse_root(0)
        sign(0)
        leave_psum(0)
        sign(1)
        square(0)
        leave_psum(1)
        inverse_root(1)
        square(1)

        signed_weight(0)
        difference(0)
        signed_weight(1)
        new_share(0)
        difference(1)
        new_share(1)
        make_step(0, "root1")
        make_step(1)
        put_back(0)
        put_back(1)
